import numpy as np
import ml_dtypes


def mxq(x, axis, fmt="e4m3"):
    dtype, down = {"e4m3": (ml_dtypes.float8_e4m3fn, 7), "e5m2": (ml_dtypes.float8_e5m2, 14)}[fmt]
    v = np.moveaxis(np.asarray(x, np.float32).astype(ml_dtypes.bfloat16).astype(np.float64), axis, -1)
    blocks = v.reshape(v.shape[:-1] + (-1, 32))
    amax = np.abs(blocks).max(-1, keepdims=True)
    byte = np.maximum(np.where(amax > 0, np.frexp(amax)[1] - 1 + 127, 0) - down, 1)
    scale = np.exp2(byte - 127.0)
    codes = (blocks / scale).astype(np.float32).astype(dtype).astype(np.float64)
    return np.moveaxis((codes * scale).reshape(v.shape), -1, axis)


WIDE = False


def mx_kscale(k):
    if not WIDE:
        return np.ones(k)
    levels = np.array([10, -10, 5, -5, 0])
    if k % 512:
        return np.exp2(np.random.permutation(np.resize(levels, k // 32))).repeat(32)
    a = np.empty((k // 512, 16))
    for p in range(k // 512):
        a[p, :8] = np.random.permutation(np.resize(levels, 8))
        for g in range(8):
            far = levels[np.abs(levels - a[p, g]) >= 10]
            a[p, g + 8] = far[np.random.randint(len(far))]
    return np.exp2(a.ravel()).repeat(32)


def f64(x):
    return np.asarray(x).astype(np.float64)


def striped(idx):
    return np.tile(idx.reshape(-1, 16).T, (8, 1)).astype(np.uint16)


def unstriped(offs):
    return offs[:16].T.reshape(-1).astype(np.int64)


E2M1 = np.array([0.0, 0.5, 1.0, 1.5, 2.0, 3.0, 4.0, 6.0, -0.0, -0.5, -1.0, -1.5, -2.0, -3.0, -4.0, -6.0])


def pack_weight(w, fmt):
    k, n = w.shape
    w = f64(np.asarray(w, np.float32).astype(ml_dtypes.bfloat16)).reshape(k // 32, 32, n)
    amax = np.abs(w).max(1)
    if fmt == "e4m3":
        byte = np.frexp(amax)[1] - 1 + 127 - 7
    else:
        mant, ex = np.frexp(amax / 6.0)
        byte = np.where(mant > 0.5, ex, ex - 1) + 127
    byte = np.clip(np.where(amax > 0, byte, 1), 1, 254)
    scaled = (w * np.exp2(127.0 - byte)[:, None, :]).reshape(k, n).astype(np.float32)
    by_word = np.ascontiguousarray(scaled.reshape(k // 512, 128, 4, n).transpose(0, 1, 3, 2))
    if fmt == "e4m3":
        words = by_word.astype(ml_dtypes.float8_e4m3fn).view(np.uint8)
    else:
        c = by_word.astype(ml_dtypes.float4_e2m1fn).view(np.uint8) & 0xF
        words = (c[..., 0::2] | (c[..., 1::2] << 4)).reshape(k // 512, 128, 2 * n)
    return np.ascontiguousarray(words), np.ascontiguousarray(byte.astype(np.uint8).reshape(k // 512, 16, n))


def unpack_weight(words, scales, fmt):
    g, _, n = scales.shape
    words = np.ascontiguousarray(words).reshape(g, 128, n, -1)
    if fmt == "e4m3":
        vals = words.view(ml_dtypes.float8_e4m3fn).astype(np.float64)
    else:
        nib = np.empty((g, 128, n, 4), np.uint8)
        nib[..., 0::2] = words & 0xF
        nib[..., 1::2] = words >> 4
        vals = E2M1[nib]
    vals = vals * np.repeat(np.exp2(scales.astype(np.float64) - 127.0), 8, axis=1)[..., None]
    return vals.transpose(0, 1, 3, 2).reshape(g * 512, n)


def gelu(v):
    return 0.5 * v * (1.0 + np.tanh(np.sqrt(2.0 / np.pi) * (v + 0.044715 * v**3)))


K, H, T, S, T3, S2, P = 1024, 1024, 4096, 1024, 2048, 512, 512

def setup_inputs():
    n = np.random.standard_normal
    s = mx_kscale(K)[:, None]
    u = mx_kscale(H)[:, None]
    d = {}
    d["tab_words"], d["tab_scales"] = pack_weight(n((K, T)) * s, "e4m3")
    d["offs"] = striped(np.random.permutation(T)[:S])
    d["tab2_words"], d["tab2_scales"] = pack_weight(n((H, T3)) / H ** 0.5 / u, "e4m3")
    d["offs2"] = striped(np.random.permutation(T3)[:S2])
    d["pos1"] = striped(np.random.permutation(S)[:P])
    d["pos2"] = striped(np.random.permutation(S)[:P])
    d["w1"] = (0.35 * n((K, H)) / K ** 0.5 / s).astype(np.float32)
    d["b1"] = np.random.uniform(-1.2, 1.2, H).astype(np.float32)
    d["w4_words"], d["w4_scales"] = pack_weight(1.3 * n((K, H)) / K ** 0.5 / s * u.T, "e2m1")
    d["rho"] = np.random.uniform(0.5, 1.5, S2).astype(np.float32)
    d["prior"] = n((S2, P)).astype(np.float32)
    return d

def reference(tab_words, tab_scales, offs, tab2_words, tab2_scales, offs2, pos1, pos2,
              w1, b1, w4_words, w4_scales, rho, prior):
    v = unpack_weight(tab_words, tab_scales, "e4m3")[:, unstriped(offs)]
    v2 = unpack_weight(tab2_words, tab2_scales, "e4m3")[:, unstriped(offs2)]
    wave = np.cos((mxq(f64(w1), 0, "e4m3").T @ v) + f64(b1)[:, None])
    h = wave * (unpack_weight(w4_words, w4_scales, "e2m1").T @ v)
    e = v2.T @ mxq(h, 0, "e4m3")
    left = e[:, unstriped(pos1)]
    right = f64(rho)[:, None] * e[:, unstriped(pos2)]
    return f64(prior) - np.abs(left - right)

@@ -1,0 +1,247 @@
+from contextlib import ExitStack
+
+import concourse.mybir as mybir
+
+K, H, T, S, T3, S2, NP = 1024, 1024, 4096, 1024, 2048, 512, 512
+FLOPS = 2 * K * H * S * 2 + 2 * H * S2 * S
+
+F32 = mybir.dt.float32
+BF16 = mybir.dt.bfloat16
+I32 = mybir.dt.int32
+U32 = mybir.dt.uint32
+U16 = mybir.dt.uint16
+U8 = mybir.dt.uint8
+FP8X4 = mybir.dt.float8_e4m3fn_x4
+FP4X4 = mybir.dt.float4_e2m1fn_x4
+ACT = mybir.ActivationFunctionType
+ALU = mybir.AluOpType
+
+P = 128
+PACK = 4
+KP = P * PACK
+N = 512
+
+
+def tile_list_fluke_lobe_scores_kernel(
+    tc, tab_words, tab_scales, offs, tab2_words, tab2_scales, offs2, pos1, pos2,
+    w1, b1, w4_words, w4_scales, rho, prior, out,
+):
+    nc = tc.nc
+    with ExitStack() as ctx:
+        lists = ctx.enter_context(tc.tile_pool(name="lists", bufs=1))
+        keep = ctx.enter_context(tc.tile_pool(name="keep", bufs=1))
+        ring = ctx.enter_context(tc.tile_pool(name="ring", bufs=3))
+        psum = ctx.enter_context(tc.psum_pool(name="psum", bufs=1))
+
+        def held(name, shape, dtype):
+            return keep.tile(shape, dtype, name=name, align_bytes=64)
+
+        offs_t = lists.tile([P, S // 16], U16, name="offs_t")
+        offs2_t = lists.tile([P, S2 // 16], U16, name="offs2_t")
+        pos1_t = lists.tile([P, NP // 16], U16, name="pos1_t")
+        pos2_t = lists.tile([P, NP // 16], U16, name="pos2_t")
+
+        tab_s = held("tab_s", [P, T], U8)
+        tab2_s = held("tab2_s", [P, T3], U8)
+        w4_s_raw = held("w4_s_raw", [P, 2, H], U8)
+        v_s1 = held("v_s1", [P, S], U8)
+        warm = held("warm", [P, 8], F32)
+        warm2 = held("warm2", [P, 8], F32)
+        nc.vector.memset(tab_s[:].bitcast(I32), 0)
+        nc.gpsimd.memset(warm[:], 0.0)
+        nc.gpsimd.memset(w4_s_raw[:].rearrange("p a c -> p (a c)").bitcast(I32), 0)
+        nc.vector.memset(v_s1[:].bitcast(I32), 0)
+        nc.gpsimd.memset(tab2_s[:].bitcast(I32), 0)
+        nc.scalar.activation(warm2[:], warm[:], ACT.Sin)
+
+        w1_raw = [[held("w1_raw%d%d" % (g, a), [P, PACK, KP], F32) for a in range(2)] for g in range(2)]
+        tab_w = [held("tab_w%d" % a, [P, T], I32) for a in range(2)]
+        tab2_w = [held("tab2_w%d" % a, [P, T3], I32) for a in range(2)]
+        w4_raw = held("w4_raw", [P, 2, 2 * H], U8)
+        b1_t = held("b1_t", [P, 2, PACK], F32)
+        rho_t = held("rho_t", [P, 4], F32)
+        prior_t = held("prior_t", [P, 4, NP], F32)
+
+        def load_w1(g, a):
+            nc.sync.dma_start(
+                w1_raw[g][a][:],
+                w1[KP * a : KP * (a + 1), KP * g : KP * (g + 1)].rearrange("(p i) c -> p i c", i=PACK),
+            )
+
+        def load_packed_scales(dst, src):
+            for q in range(4):
+                nc.sync.dma_start(dst[32 * q : 32 * q + 8, :].bitcast(I32), src[:, 4 * q : 4 * q + 4, :].bitcast(I32))
+
+        def load_words(dst, src):
+            nc.sync.dma_start(dst[:], src.rearrange("p t i -> p (t i)").bitcast(I32))
+
+        nc.sync.dma_start(offs_t[:], offs)
+        load_w1(0, 0)
+        load_packed_scales(tab_s, tab_scales)
+        load_w1(0, 1)
+        nc.sync.dma_start(w4_raw[:].bitcast(I32), w4_words.rearrange("a p c -> p a c").bitcast(I32))
+        for q in range(4):
+            nc.sync.dma_start(
+                w4_s_raw[32 * q : 32 * q + 4, :, :].bitcast(I32),
+                w4_scales[:, 4 * q : 4 * q + 4, :].rearrange("a r c -> r a c").bitcast(I32),
+            )
+        load_words(tab_w[0], tab_words[0])
+        nc.sync.dma_start(b1_t[:], b1.rearrange("(g p t) -> p g t", g=2, t=PACK))
+        load_words(tab_w[1], tab_words[1])
+        load_w1(1, 0)
+        load_w1(1, 1)
+        nc.sync.dma_start(offs2_t[:], offs2)
+        load_packed_scales(tab2_s, tab2_scales)
+        load_words(tab2_w[0], tab2_words[0])
+        load_words(tab2_w[1], tab2_words[1])
+        nc.sync.dma_start(pos2_t[:], pos2)
+        nc.sync.dma_start(pos1_t[:], pos1)
+        with nc.allow_non_contiguous_dma(reason="one value a partition"):
+            nc.sync.dma_start(rho_t[:], rho.rearrange("(c p) -> p c", p=P))
+        nc.sync.dma_start(prior_t[:], prior.rearrange("(c p) n -> p c n", p=P))
+
+        w1_q = [[held("w1_q%d%d" % (g, a), [P, KP], U32) for a in range(2)] for g in range(2)]
+        w1_s = [[held("w1_s%d%d" % (g, a), [P, KP], U8) for a in range(2)] for g in range(2)]
+        w1_b = [[held("w1_b%d%d" % (g, a), [P, PACK * KP], BF16) for a in range(2)] for g in range(2)]
+
+        def cast_w1(g, a, on_scalar):
+            dst = w1_b[g][a][:].rearrange("p (t m i) -> p m t i", t=PACK, i=PACK)
+            src = w1_raw[g][a][:].rearrange("p i (m t) -> p m t i", t=PACK)
+            if on_scalar:
+                nc.scalar.copy(dst, src)
+            else:
+                nc.vector.tensor_copy(dst, src)
+
+        def quant_w1(g, a):
+            nc.vector.quantize_mx(out=w1_q[g][a][:].bitcast(FP8X4), scales=w1_s[g][a][:], in_=w1_b[g][a][:])
+
+        v_s = held("v_s", [P, S], U8)
+        v_w0 = held("v_w0", [P, S], U32)
+        v_w1 = [held("v_w1%d" % jh, [P, N], U32) for jh in range(2)]
+        w4_p = held("w4_p", [P, 2, 2 * H], U8)
+        w4_s = held("w4_s", [P, 2 * H], U8)
+        half_b = held("half_b", [P, 2 * PACK], F32)
+
+        cast_w1(0, 0, True)
+        nc.vector.tensor_copy(v_s[:], tab_s[:].indirect(offs_t[:]))
+        for q in range(4):
+            nc.scalar.dma_start(v_s1[32 * q : 32 * q + 4, :].bitcast(I32), v_s[32 * q + 4 : 32 * q + 8, :].bitcast(I32))
+        cast_w1(0, 1, True)
+        for a in range(2):
+            nc.vector.tensor_copy(
+                w4_p[:, a, :].rearrange("p (g t m b) -> p g m t b", g=2, t=PACK, b=2),
+                w4_raw[:, a, :].rearrange("p (g m t b) -> p g m t b", g=2, t=PACK, b=2),
+            )
+        quant_w1(0, 0)
+        nc.vector.tensor_copy(
+            w4_s[:].rearrange("p (u t m) -> p u m t", u=4, t=PACK),
+            w4_s_raw[:].rearrange("p a (g m t) -> p (a g) m t", g=2, t=PACK),
+        )
+        quant_w1(0, 1)
+        nc.vector.tensor_copy(v_w0[:], tab_w[0][:].bitcast(U32).indirect(offs_t[:]))
+        nc.vector.tensor_scalar(half_b[:], b1_t[:].rearrange("p g t -> p (g t)"), 0.5, None, ALU.mult)
+        for jh in range(2):
+            nc.vector.tensor_copy(v_w1[jh][:], tab_w[1][:].bitcast(U32).indirect(offs_t[:, 32 * jh : 32 * (jh + 1)]))
+
+        v2_w = [held("v2_w%d" % a, [P, S2], U32) for a in range(2)]
+        v2_s = held("v2_s", [P, S2], U8)
+        h_q = [[held("h_q%d%d" % (g, jh), [P, N], U32) for jh in range(2)] for g in range(2)]
+        h_s = [[held("h_s%d%d" % (g, jh), [P, N], U8) for jh in range(2)] for g in range(2)]
+        e_t = [held("e_t%d" % c, [P, S], F32) for c in range(4)]
+
+        def v_words(a, jh):
+            return (v_w0[:, N * jh : N * (jh + 1)] if a == 0 else v_w1[jh][:]).bitcast(FP8X4)
+
+        def unit(g, jh, t, planes):
+            js = slice(N * jh, N * (jh + 1))
+            ms = slice(P * t, P * (t + 1))
+            pa = psum.tile([P, N], F32, name="pa", bufs=3)
+            pb = psum.tile([P, N], F32, name="pb", bufs=3)
+            for a in range(2):
+                nc.tensor.matmul_mx(
+                    out=pa[:], lhsT=w1_q[g][a][:, ms].bitcast(FP8X4), lhsT_scale=w1_s[g][a][:, ms],
+                    rhs=v_words(a, jh), rhs_scale=v_s[4 * a :, js], start=(a == 0), stop=(a == 1),
+                )
+            for a in range(2):
+                col = H * a + KP * g + P * t
+                nc.tensor.matmul_mx(
+                    out=pb[:], lhsT=w4_p[:, a, 2 * (KP * g + P * t) : 2 * (KP * g + P * (t + 1))].bitcast(FP4X4),
+                    lhsT_scale=w4_s[:, col : col + P],
+                    rhs=v_words(a, jh), rhs_scale=(v_s if a == 0 else v_s1)[:, js], start=(a == 0), stop=(a == 1),
+                )
+            sn = ring.tile([P, N], F32, name="sn")
+            nc.scalar.activation(sn[:], pa[:], ACT.Sin, bias=half_b[:, PACK * g + t : PACK * g + t + 1], scale=0.5)
+            sq = ring.tile([P, N], F32, name="sq")
+            nc.scalar.activation(sq[:], sn[:], ACT.Square)
+            nc.vector.scalar_tensor_tensor(planes[:, t, :], sq[:], 0.5, pb[:], ALU.subtract, ALU.mult)
+
+        def finish(g, jh, planes):
+            woven = ring.tile([P, PACK * N], BF16, name="woven", bufs=2, align_bytes=64)
+            nc.vector.tensor_copy(
+                woven[:].rearrange("p (c i t) -> p c t i", i=8, t=PACK),
+                planes[:].rearrange("p t (c i) -> p c t i", i=8),
+            )
+            nc.vector.quantize_mx(out=h_q[g][jh][:].bitcast(FP8X4), scales=h_s[g][jh][:], in_=woven[:])
+
+        def quarter(g, jh):
+            planes = ring.tile([P, PACK, N], BF16, name="planes", bufs=2, align_bytes=64)
+            for t in range(PACK):
+                unit(g, jh, t, planes)
+            return planes
+
+        def scores(c, jh):
+            pe = psum.tile([P, N], F32, name="pe", bufs=2)
+            ms = slice(P * c, P * (c + 1))
+            for a in range(2):
+                nc.tensor.matmul_mx(
+                    out=pe[:], lhsT=v2_w[a][:, ms].bitcast(FP8X4), lhsT_scale=v2_s[4 * a :, ms],
+                    rhs=h_q[a][jh][:].bitcast(FP8X4), rhs_scale=h_s[a][jh][:], start=(a == 0), stop=(a == 1),
+                )
+            nc.scalar.copy(e_t[c][:, N * jh : N * (jh + 1)], pe[:])
+
+        p00 = quarter(0, 0)
+        cast_w1(1, 0, False)
+        quant_w1(1, 0)
+        p01 = quarter(0, 1)
+        finish(0, 0, p00)
+        cast_w1(1, 1, False)
+        quant_w1(1, 1)
+        p10 = quarter(1, 0)
+        finish(0, 1, p01)
+        nc.vector.tensor_copy(v2_s[:], tab2_s[:].indirect(offs2_t[:]))
+        for a in range(2):
+            nc.vector.tensor_copy(v2_w[a][:], tab2_w[a][:].bitcast(U32).indirect(offs2_t[:]))
+        finish(1, 0, p10)
+        p11 = quarter(1, 1)
+        for c in range(4):
+            scores(c, 0)
+        finish(1, 1, p11)
+
+        right = [None] * 4
+        dist = [None] * 4
+
+        def pick_right(c):
+            scores(c, 1)
+            r = ring.tile([P, NP], F32, name="r", bufs=2)
+            nc.vector.tensor_copy(r[:], e_t[c][:].indirect(pos2_t[:]))
+            right[c] = ring.tile([P, NP], F32, name="rr")
+            nc.scalar.activation(right[c][:], r[:], ACT.Copy, scale=rho_t[:, c : c + 1])
+
+        def pick_left(c):
+            d = ring.tile([P, NP], F32, name="d", bufs=2)
+            nc.vector.tensor_tensor(d[:], e_t[c][:].indirect(pos1_t[:]), right[c][:], ALU.subtract)
+            dist[c] = ring.tile([P, NP], F32, name="dd")
+            nc.scalar.activation(dist[c][:], d[:], ACT.Abs, scale=2.0)
+
+        def store(c):
+            o = ring.tile([P, NP], F32, name="o", bufs=2)
+            nc.vector.tensor_tensor(o[:], prior_t[:, c, :], dist[c][:], ALU.subtract)
+            nc.sync.dma_start(out[P * c : P * (c + 1), :], o[:])
+
+        for step in range(6):
+            if step < 4:
+                pick_right(step)
+            if 1 <= step < 5:
+                pick_left(step - 1)
+            if step >= 2:
+                store(step - 2)

@@ -41,78 +41,73 @@ def tile_list_fluke_lobe_scores_kernel(
         pos1_t = lists.tile([P, NP // 16], U16, name="pos1_t")
         pos2_t = lists.tile([P, NP // 16], U16, name="pos2_t")
 
-        tab_s = held("tab_s", [P, T], U8)
-        tab2_s = held("tab2_s", [P, T3], U8)
-        w4_s_raw = held("w4_s_raw", [P, 2, H], U8)
-        v_s1 = held("v_s1", [P, S], U8)
-        warm = held("warm", [P, 8], F32)
+        def shared(name, tag, shape, dtype):
+            return keep.tile(shape, dtype, name=name, tag=tag, align_bytes=64)
+
+        tab_s = shared("tab_s", "x0", [P, T], U8)
+        warm = shared("warm", "x2", [P, 8], F32)
         warm2 = held("warm2", [P, 8], F32)
+        v_s1 = held("v_s1", [P, S], U8)
         nc.vector.memset(tab_s[:].bitcast(I32), 0)
-        nc.gpsimd.memset(warm[:], 0.0)
-        nc.gpsimd.memset(w4_s_raw[:].rearrange("p a c -> p (a c)").bitcast(I32), 0)
+        nc.vector.memset(warm[:], 0.0)
         nc.vector.memset(v_s1[:].bitcast(I32), 0)
-        nc.gpsimd.memset(tab2_s[:].bitcast(I32), 0)
         nc.scalar.activation(warm2[:], warm[:], ACT.Sin)
 
-        w1_raw = [[held("w1_raw%d%d" % (g, a), [P, PACK, KP], F32) for a in range(2)] for g in range(2)]
-        tab_w = [held("tab_w%d" % a, [P, T], I32) for a in range(2)]
-        tab2_w = [held("tab2_w%d" % a, [P, T3], I32) for a in range(2)]
-        w4_raw = held("w4_raw", [P, 2, 2 * H], U8)
-        b1_t = held("b1_t", [P, 2, PACK], F32)
-        rho_t = held("rho_t", [P, 4], F32)
-        prior_t = held("prior_t", [P, 4, NP], F32)
+        w1_raw = {}
+        tab_w = {}
+        w4_raw = shared("w4_raw", "x1", [P, 2, 2 * H], U8)
+        b1_t = shared("b1_t", "x5", [P, 2, PACK], F32)
 
-        def load_w1(g, a):
+        def load_w1(g, a, tag):
+            w1_raw[g, a] = shared("w1_raw%d%d" % (g, a), tag, [P, PACK, KP], F32)
             nc.sync.dma_start(
-                w1_raw[g][a][:],
+                w1_raw[g, a][:],
                 w1[KP * a : KP * (a + 1), KP * g : KP * (g + 1)].rearrange("(p i) c -> p i c", i=PACK),
             )
 
-        def load_packed_scales(dst, src):
-            for q in range(4):
-                nc.sync.dma_start(dst[32 * q : 32 * q + 8, :].bitcast(I32), src[:, 4 * q : 4 * q + 4, :].bitcast(I32))
+        def load_words(a, tag):
+            tab_w[a] = shared("tab_w%d" % a, tag, [P, T], I32)
+            nc.sync.dma_start(tab_w[a][:], tab_words[a].rearrange("p t i -> p (t i)").bitcast(I32))
 
-        def load_words(dst, src):
-            nc.sync.dma_start(dst[:], src.rearrange("p t i -> p (t i)").bitcast(I32))
+        tab2_w = {}
+
+        def load_words2(a, tag):
+            tab2_w[a] = shared("tab2_w%d" % a, tag, [P, T3], I32)
+            nc.sync.dma_start(tab2_w[a][:], tab2_words[a].rearrange("p t i -> p (t i)").bitcast(I32))
+
+        def load_scale_rows(queue, dst, src):
+            for q in range(4):
+                queue.dma_start(
+                    dst[32 * q : 32 * q + 4, :].rearrange("r (a c) -> r a c", a=2).bitcast(I32),
+                    src[:, 4 * q : 4 * q + 4, :].rearrange("a r c -> r a c").bitcast(I32),
+                )
 
         nc.sync.dma_start(offs_t[:], offs)
-        load_w1(0, 0)
-        load_packed_scales(tab_s, tab_scales)
-        load_w1(0, 1)
-        nc.sync.dma_start(w4_raw[:].bitcast(I32), w4_words.rearrange("a p c -> p a c").bitcast(I32))
-        for q in range(4):
-            nc.sync.dma_start(
-                w4_s_raw[32 * q : 32 * q + 4, :, :].bitcast(I32),
-                w4_scales[:, 4 * q : 4 * q + 4, :].rearrange("a r c -> r a c").bitcast(I32),
-            )
-        load_words(tab_w[0], tab_words[0])
-        nc.sync.dma_start(b1_t[:], b1.rearrange("(g p t) -> p g t", g=2, t=PACK))
-        load_words(tab_w[1], tab_words[1])
-        load_w1(1, 0)
-        load_w1(1, 1)
+        nc.scalar.dma_start(b1_t[:], b1.rearrange("(g p t) -> p g t", g=2, t=PACK))
         nc.sync.dma_start(offs2_t[:], offs2)
-        load_packed_scales(tab2_s, tab2_scales)
-        load_words(tab2_w[0], tab2_words[0])
-        load_words(tab2_w[1], tab2_words[1])
-        nc.sync.dma_start(pos2_t[:], pos2)
         nc.sync.dma_start(pos1_t[:], pos1)
-        with nc.allow_non_contiguous_dma(reason="one value a partition"):
-            nc.sync.dma_start(rho_t[:], rho.rearrange("(c p) -> p c", p=P))
-        nc.sync.dma_start(prior_t[:], prior.rearrange("(c p) n -> p c n", p=P))
+        nc.sync.dma_start(pos2_t[:], pos2)
+        nc.sync.dma_start(w4_raw[:].bitcast(I32), w4_words.rearrange("a p c -> p a c").bitcast(I32))
+        load_w1(0, 0, "x3")
+        load_w1(0, 1, "x4")
+        for q in range(4):
+            nc.sync.dma_start(tab_s[32 * q : 32 * q + 8, :].bitcast(I32), tab_scales[:, 4 * q : 4 * q + 4, :].bitcast(I32))
 
-        w1_q = [[held("w1_q%d%d" % (g, a), [P, KP], U32) for a in range(2)] for g in range(2)]
+        w1_q = [[None, None], [None, None]]
         w1_s = [[held("w1_s%d%d" % (g, a), [P, KP], U8) for a in range(2)] for g in range(2)]
-        w1_b = [[held("w1_b%d%d" % (g, a), [P, PACK * KP], BF16) for a in range(2)] for g in range(2)]
+        w1_b = [[None, None], [None, None]]
 
         def cast_w1(g, a, on_scalar):
+            w1_b[g][a] = shared("w1_b%d%d" % (g, a), "w1_b%d" % a if g == 0 else "w1_b1%d" % a, [P, PACK * KP], BF16)
             dst = w1_b[g][a][:].rearrange("p (t m i) -> p m t i", t=PACK, i=PACK)
-            src = w1_raw[g][a][:].rearrange("p i (m t) -> p m t i", t=PACK)
+            src = w1_raw[g, a][:].rearrange("p i (m t) -> p m t i", t=PACK)
             if on_scalar:
                 nc.scalar.copy(dst, src)
             else:
                 nc.vector.tensor_copy(dst, src)
 
         def quant_w1(g, a):
+            w1_q[g][a] = shared("w1_q%d%d" % (g, a), "x0" if (g, a) == (0, 1) else "w1_q%d%d" % (g, a), [P, KP], U32)
             nc.vector.quantize_mx(out=w1_q[g][a][:].bitcast(FP8X4), scales=w1_s[g][a][:], in_=w1_b[g][a][:])
 
         v_s = held("v_s", [P, S], U8)
@@ -122,26 +117,45 @@ def tile_list_fluke_lobe_scores_kernel(
         w4_s = held("w4_s", [P, 2 * H], U8)
         half_b = held("half_b", [P, 2 * PACK], F32)
 
-        cast_w1(0, 0, True)
-        nc.vector.tensor_copy(v_s[:], tab_s[:].indirect(offs_t[:]))
-        for q in range(4):
-            nc.scalar.dma_start(v_s1[32 * q : 32 * q + 4, :].bitcast(I32), v_s[32 * q + 4 : 32 * q + 8, :].bitcast(I32))
-        cast_w1(0, 1, True)
+        nc.vector.tensor_scalar(half_b[:], b1_t[:].rearrange("p g t -> p (g t)"), 0.5, None, ALU.mult)
+        load_words(0, "x2")
+        w4_s_raw = shared("w4_s_raw", "x5", [P, 2 * H], U8)
+        nc.vector.memset(w4_s_raw[:].bitcast(I32), 0)
+        load_scale_rows(nc.sync, w4_s_raw, w4_scales)
         for a in range(2):
             nc.vector.tensor_copy(
                 w4_p[:, a, :].rearrange("p (g t m b) -> p g m t b", g=2, t=PACK, b=2),
                 w4_raw[:, a, :].rearrange("p (g m t b) -> p g m t b", g=2, t=PACK, b=2),
             )
+        cast_w1(0, 0, True)
+        load_words(1, "x3")
+        cast_w1(0, 1, True)
         quant_w1(0, 0)
-        nc.vector.tensor_copy(
-            w4_s[:].rearrange("p (u t m) -> p u m t", u=4, t=PACK),
-            w4_s_raw[:].rearrange("p a (g m t) -> p (a g) m t", g=2, t=PACK),
-        )
+        load_w1(1, 0, "w1_b0")
+        load_words2(0, "x4")
+        nc.vector.tensor_copy(v_s[:], tab_s[:].indirect(offs_t[:]))
+        for q in range(4):
+            nc.sync.dma_start(v_s1[32 * q : 32 * q + 4, :].bitcast(I32), v_s[32 * q + 4 : 32 * q + 8, :].bitcast(I32))
         quant_w1(0, 1)
+        load_w1(1, 1, "w1_b1")
         nc.vector.tensor_copy(v_w0[:], tab_w[0][:].bitcast(U32).indirect(offs_t[:]))
-        nc.vector.tensor_scalar(half_b[:], b1_t[:].rearrange("p g t -> p (g t)"), 0.5, None, ALU.mult)
+        load_words2(1, "x2")
+        def deal_w4_scales(g):
+            nc.vector.tensor_copy(
+                w4_s[:].rearrange("p (a g t m) -> p g a m t", a=2, g=2, t=PACK)[:, g],
+                w4_s_raw[:].rearrange("p (a g m t) -> p g a m t", a=2, g=2, t=PACK)[:, g],
+            )
+
+        deal_w4_scales(0)
         for jh in range(2):
             nc.vector.tensor_copy(v_w1[jh][:], tab_w[1][:].bitcast(U32).indirect(offs_t[:, 32 * jh : 32 * (jh + 1)]))
+        deal_w4_scales(1)
+        tab2_s = shared("tab2_s", "x5", [P, T3], U8)
+        nc.vector.memset(tab2_s[:].bitcast(I32), 0)
+        for q in range(4):
+            nc.sync.dma_start(tab2_s[32 * q : 32 * q + 8, :].bitcast(I32), tab2_scales[:, 4 * q : 4 * q + 4, :].bitcast(I32))
+        prior_t = shared("prior_t", "x3", [P, 4, NP], F32)
+        nc.sync.dma_start(prior_t[:], prior.rearrange("(c p) n -> p c n", p=P))
 
         v2_w = [held("v2_w%d" % a, [P, S2], U32) for a in range(2)]
         v2_s = held("v2_s", [P, S2], U8)
@@ -152,16 +166,30 @@ def tile_list_fluke_lobe_scores_kernel(
         def v_words(a, jh):
             return (v_w0[:, N * jh : N * (jh + 1)] if a == 0 else v_w1[jh][:]).bitcast(FP8X4)
 
-        def unit(g, jh, t, planes):
+        UNITS = [(g, jh, t) for g in range(2) for jh in range(2) for t in range(PACK)]
+        sines, squares, prods, planes, woven = {}, {}, {}, {}, {}
+
+        def phase(u):
+            g, jh, t = UNITS[u]
             js = slice(N * jh, N * (jh + 1))
             ms = slice(P * t, P * (t + 1))
             pa = psum.tile([P, N], F32, name="pa", bufs=3)
-            pb = psum.tile([P, N], F32, name="pb", bufs=3)
             for a in range(2):
                 nc.tensor.matmul_mx(
                     out=pa[:], lhsT=w1_q[g][a][:, ms].bitcast(FP8X4), lhsT_scale=w1_s[g][a][:, ms],
                     rhs=v_words(a, jh), rhs_scale=v_s[4 * a :, js], start=(a == 0), stop=(a == 1),
                 )
+            sines[u] = ring.tile([P, N], F32, name="sn", bufs=3)
+            nc.scalar.activation(sines[u][:], pa[:], ACT.Sin, bias=half_b[:, PACK * g + t : PACK * g + t + 1], scale=0.5)
+
+        def square(u):
+            squares[u] = ring.tile([P, N], F32, name="sq", bufs=6)
+            nc.scalar.activation(squares[u][:], sines[u][:], ACT.Square)
+
+        def amplitude(u):
+            g, jh, t = UNITS[u]
+            js = slice(N * jh, N * (jh + 1))
+            pb = psum.tile([P, N], F32, name="pb", bufs=3)
             for a in range(2):
                 col = H * a + KP * g + P * t
                 nc.tensor.matmul_mx(
@@ -169,79 +197,116 @@ def tile_list_fluke_lobe_scores_kernel(
                     lhsT_scale=w4_s[:, col : col + P],
                     rhs=v_words(a, jh), rhs_scale=(v_s if a == 0 else v_s1)[:, js], start=(a == 0), stop=(a == 1),
                 )
-            sn = ring.tile([P, N], F32, name="sn")
-            nc.scalar.activation(sn[:], pa[:], ACT.Sin, bias=half_b[:, PACK * g + t : PACK * g + t + 1], scale=0.5)
-            sq = ring.tile([P, N], F32, name="sq")
-            nc.scalar.activation(sq[:], sn[:], ACT.Square)
-            nc.vector.scalar_tensor_tensor(planes[:, t, :], sq[:], 0.5, pb[:], ALU.subtract, ALU.mult)
+            prods[u] = pb
 
-        def finish(g, jh, planes):
-            woven = ring.tile([P, PACK * N], BF16, name="woven", bufs=2, align_bytes=64)
+        def combine(u):
+            g, jh, t = UNITS[u]
+            if t == 0:
+                planes[2 * g + jh] = ring.tile([P, PACK, N], BF16, name="planes", bufs=2, align_bytes=64)
+            nc.vector.scalar_tensor_tensor(planes[2 * g + jh][:, t, :], squares[u][:], 0.5, prods[u][:], ALU.subtract, ALU.mult)
+
+        def weave(q, j0=0, j1=N):
+            if j0 == 0:
+                woven[q] = ring.tile([P, PACK * N], BF16, name="woven", bufs=2, align_bytes=64)
             nc.vector.tensor_copy(
-                woven[:].rearrange("p (c i t) -> p c t i", i=8, t=PACK),
-                planes[:].rearrange("p t (c i) -> p c t i", i=8),
+                woven[q][:, PACK * j0 : PACK * j1].rearrange("p (c i t) -> p c t i", i=8, t=PACK),
+                planes[q][:, :, j0:j1].rearrange("p t (c i) -> p c t i", i=8),
             )
-            nc.vector.quantize_mx(out=h_q[g][jh][:].bitcast(FP8X4), scales=h_s[g][jh][:], in_=woven[:])
 
-        def quarter(g, jh):
-            planes = ring.tile([P, PACK, N], BF16, name="planes", bufs=2, align_bytes=64)
-            for t in range(PACK):
-                unit(g, jh, t, planes)
-            return planes
+        def quant_h(q, j0=0, j1=N):
+            g, jh = divmod(q, 2)
+            nc.vector.quantize_mx(
+                out=h_q[g][jh][:, j0:j1].bitcast(FP8X4), scales=h_s[g][jh][:, j0:j1], in_=woven[q][:, PACK * j0 : PACK * j1]
+            )
 
-        def scores(c, jh):
-            pe = psum.tile([P, N], F32, name="pe", bufs=2)
+        def gather_v2(a):
+            nc.vector.tensor_copy(v2_w[a][:], tab2_w[a][:].bitcast(U32).indirect(offs2_t[:]))
+
+        def gather_v2_s():
+            nc.vector.tensor_copy(v2_s[:], tab2_s[:].indirect(offs2_t[:]))
+
+        def scores(c, jh, on_scalar, j0=0, j1=N):
+            pe = psum.tile([P, j1 - j0], F32, name="pe", bufs=2)
             ms = slice(P * c, P * (c + 1))
             for a in range(2):
                 nc.tensor.matmul_mx(
                     out=pe[:], lhsT=v2_w[a][:, ms].bitcast(FP8X4), lhsT_scale=v2_s[4 * a :, ms],
-                    rhs=h_q[a][jh][:].bitcast(FP8X4), rhs_scale=h_s[a][jh][:], start=(a == 0), stop=(a == 1),
+                    rhs=h_q[a][jh][:, j0:j1].bitcast(FP8X4), rhs_scale=h_s[a][jh][:, j0:j1], start=(a == 0), stop=(a == 1),
                 )
-            nc.scalar.copy(e_t[c][:, N * jh : N * (jh + 1)], pe[:])
+            if on_scalar:
+                nc.scalar.copy(e_t[c][:, N * jh + j0 : N * jh + j1], pe[:])
+            else:
+                nc.vector.tensor_copy(e_t[c][:, N * jh + j0 : N * jh + j1], pe[:])
 
-        p00 = quarter(0, 0)
-        cast_w1(1, 0, False)
-        quant_w1(1, 0)
-        p01 = quarter(0, 1)
-        finish(0, 0, p00)
-        cast_w1(1, 1, False)
-        quant_w1(1, 1)
-        p10 = quarter(1, 0)
-        finish(0, 1, p01)
-        nc.vector.tensor_copy(v2_s[:], tab2_s[:].indirect(offs2_t[:]))
-        for a in range(2):
-            nc.vector.tensor_copy(v2_w[a][:], tab2_w[a][:].bitcast(U32).indirect(offs2_t[:]))
-        finish(1, 0, p10)
-        p11 = quarter(1, 1)
-        for c in range(4):
-            scores(c, 0)
-        finish(1, 1, p11)
+        half = N // 2
+        extras = {
+            0: [lambda: cast_w1(1, 0, False)],
+            1: [lambda: quant_w1(1, 0), lambda: cast_w1(1, 1, True)],
+            2: [lambda: gather_v2(0)],
+            3: [lambda: quant_w1(1, 1)],
+            4: [lambda: weave(0)],
+            5: [lambda: quant_h(0)],
+            6: [lambda: gather_v2(1)],
+            8: [lambda: weave(1)],
+            9: [lambda: quant_h(1)],
+            10: [gather_v2_s],
+            12: [lambda: weave(2)],
+            13: [lambda: quant_h(2)],
+            14: [lambda: scores(0, 0, True), lambda: scores(1, 0, True)],
+            15: [lambda: weave(3, 0, half), lambda: weave(3, half, N), lambda: quant_h(3, 0, half), lambda: scores(0, 1, True, 0, half),
+                 lambda: quant_h(3, half, N), lambda: scores(0, 1, True, half, N)],
+        }
+        LEAD = 4
+        for step in range(-LEAD, 16):
+            if step + LEAD < 16:
+                phase(step + LEAD)
+            if 0 <= step + LEAD - 1 < 16:
+                square(step + LEAD - 1)
+            if 0 <= step + 1 < 16:
+                amplitude(step + 1)
+            if step >= 0:
+                combine(step)
+                for f in extras.get(step, []):
+                    f()
 
-        right = [None] * 4
-        dist = [None] * 4
+        rho_t = shared("rho_t", "w1_b10", [P, 4], F32)
+        with nc.allow_non_contiguous_dma(reason="one value a partition"):
+            nc.sync.dma_start(rho_t[:], rho.rearrange("(c p) -> p c", p=P))
+        picked, right, diff, dist = {}, {}, {}, {}
 
         def pick_right(c):
-            scores(c, 1)
-            r = ring.tile([P, NP], F32, name="r", bufs=2)
-            nc.vector.tensor_copy(r[:], e_t[c][:].indirect(pos2_t[:]))
+            picked[c] = ring.tile([P, NP], F32, name="r", bufs=2)
+            nc.vector.tensor_copy(picked[c][:], e_t[c][:].indirect(pos2_t[:]))
+
+        def balance(c):
             right[c] = ring.tile([P, NP], F32, name="rr")
-            nc.scalar.activation(right[c][:], r[:], ACT.Copy, scale=rho_t[:, c : c + 1])
+            nc.scalar.activation(right[c][:], picked[c][:], ACT.Copy, scale=rho_t[:, c : c + 1])
 
         def pick_left(c):
-            d = ring.tile([P, NP], F32, name="d", bufs=2)
-            nc.vector.tensor_tensor(d[:], e_t[c][:].indirect(pos1_t[:]), right[c][:], ALU.subtract)
+            diff[c] = ring.tile([P, NP], F32, name="d", bufs=2)
+            nc.vector.tensor_tensor(diff[c][:], e_t[c][:].indirect(pos1_t[:]), right[c][:], ALU.subtract)
+
+        def distance(c):
             dist[c] = ring.tile([P, NP], F32, name="dd")
-            nc.scalar.activation(dist[c][:], d[:], ACT.Abs, scale=2.0)
+            nc.scalar.activation(dist[c][:], diff[c][:], ACT.Abs, scale=2.0)
 
         def store(c):
             o = ring.tile([P, NP], F32, name="o", bufs=2)
             nc.vector.tensor_tensor(o[:], prior_t[:, c, :], dist[c][:], ALU.subtract)
             nc.sync.dma_start(out[P * c : P * (c + 1), :], o[:])
 
-        for step in range(6):
-            if step < 4:
-                pick_right(step)
-            if 1 <= step < 5:
-                pick_left(step - 1)
-            if step >= 2:
-                store(step - 2)
+        pick_right(0)
+        for c in range(6):
+            if c + 1 < 4:
+                if c + 1 >= 2:
+                    scores(c + 1, 0, True)
+                scores(c + 1, 1, True)
+                pick_right(c + 1)
+            if c < 4:
+                balance(c)
+            if 1 <= c < 5:
+                distance(c - 1)
+            if c < 4:
+                pick_left(c)
+            if 1 <= c < 5:
+                store(c - 1)

from contextlib import ExitStack

import concourse.mybir as mybir

K, H, T, S, T3, S2, NP = 1024, 1024, 4096, 1024, 2048, 512, 512
FLOPS = 2 * K * H * S * 2 + 2 * H * S2 * S

F32 = mybir.dt.float32
BF16 = mybir.dt.bfloat16
I32 = mybir.dt.int32
U32 = mybir.dt.uint32
U16 = mybir.dt.uint16
U8 = mybir.dt.uint8
FP8X4 = mybir.dt.float8_e4m3fn_x4
FP4X4 = mybir.dt.float4_e2m1fn_x4
ACT = mybir.ActivationFunctionType
ALU = mybir.AluOpType

P = 128
PACK = 4
KP = P * PACK
N = 512


def tile_list_fluke_lobe_scores_kernel(
    tc, tab_words, tab_scales, offs, tab2_words, tab2_scales, offs2, pos1, pos2,
    w1, b1, w4_words, w4_scales, rho, prior, out,
):
    nc = tc.nc
    with ExitStack() as ctx:
        lists = ctx.enter_context(tc.tile_pool(name="lists", bufs=1))
        keep = ctx.enter_context(tc.tile_pool(name="keep", bufs=1))
        ring = ctx.enter_context(tc.tile_pool(name="ring", bufs=3))
        psum = ctx.enter_context(tc.psum_pool(name="psum", bufs=1))

        def held(name, shape, dtype):
            return keep.tile(shape, dtype, name=name, align_bytes=64)

        offs_t = lists.tile([P, S // 16], U16, name="offs_t")
        offs2_t = lists.tile([P, S2 // 16], U16, name="offs2_t")
        pos1_t = lists.tile([P, NP // 16], U16, name="pos1_t")
        pos2_t = lists.tile([P, NP // 16], U16, name="pos2_t")

        def shared(name, tag, shape, dtype):
            return keep.tile(shape, dtype, name=name, tag=tag, align_bytes=64)

        tab_s = shared("tab_s", "x0", [P, T], U8)
        warm = shared("warm", "x2", [P, 8], F32)
        warm2 = held("warm2", [P, 8], F32)
        v_s1 = held("v_s1", [P, S], U8)
        nc.vector.memset(tab_s[:].bitcast(I32), 0)
        nc.vector.memset(warm[:], 0.0)
        nc.vector.memset(v_s1[:].bitcast(I32), 0)
        nc.scalar.activation(warm2[:], warm[:], ACT.Sin)

        w1_raw = {}
        tab_w = {}
        w4_raw = shared("w4_raw", "x1", [P, 2, 2 * H], U8)
        b1_t = shared("b1_t", "x5", [P, 2, PACK], F32)

        def load_w1(g, a, tag):
            w1_raw[g, a] = shared("w1_raw%d%d" % (g, a), tag, [P, PACK, KP], F32)
            nc.sync.dma_start(
                w1_raw[g, a][:],
                w1[KP * a : KP * (a + 1), KP * g : KP * (g + 1)].rearrange("(p i) c -> p i c", i=PACK),
            )

        def load_words(a, tag):
            tab_w[a] = shared("tab_w%d" % a, tag, [P, T], I32)
            nc.sync.dma_start(tab_w[a][:], tab_words[a].rearrange("p t i -> p (t i)").bitcast(I32))

        tab2_w = {}

        def load_words2(a, tag):
            tab2_w[a] = shared("tab2_w%d" % a, tag, [P, T3], I32)
            nc.sync.dma_start(tab2_w[a][:], tab2_words[a].rearrange("p t i -> p (t i)").bitcast(I32))

        def load_scale_rows(queue, dst, src):
            for q in range(4):
                queue.dma_start(
                    dst[32 * q : 32 * q + 4, :].rearrange("r (a c) -> r a c", a=2).bitcast(I32),
                    src[:, 4 * q : 4 * q + 4, :].rearrange("a r c -> r a c").bitcast(I32),
                )

        nc.sync.dma_start(offs_t[:], offs)
        nc.scalar.dma_start(b1_t[:], b1.rearrange("(g p t) -> p g t", g=2, t=PACK))
        nc.sync.dma_start(offs2_t[:], offs2)
        nc.sync.dma_start(pos1_t[:], pos1)
        nc.sync.dma_start(pos2_t[:], pos2)
        nc.sync.dma_start(w4_raw[:].bitcast(I32), w4_words.rearrange("a p c -> p a c").bitcast(I32))
        load_w1(0, 0, "x3")
        load_w1(0, 1, "x4")
        for q in range(4):
            nc.sync.dma_start(tab_s[32 * q : 32 * q + 8, :].bitcast(I32), tab_scales[:, 4 * q : 4 * q + 4, :].bitcast(I32))

        w1_q = [[None, None], [None, None]]
        w1_s = [[held("w1_s%d%d" % (g, a), [P, KP], U8) for a in range(2)] for g in range(2)]
        w1_b = [[None, None], [None, None]]

        def cast_w1(g, a, on_scalar):
            w1_b[g][a] = shared("w1_b%d%d" % (g, a), "w1_b%d" % a if g == 0 else "w1_b1%d" % a, [P, PACK * KP], BF16)
            dst = w1_b[g][a][:].rearrange("p (t m i) -> p m t i", t=PACK, i=PACK)
            src = w1_raw[g, a][:].rearrange("p i (m t) -> p m t i", t=PACK)
            if on_scalar:
                nc.scalar.copy(dst, src)
            else:
                nc.vector.tensor_copy(dst, src)

        def quant_w1(g, a):
            w1_q[g][a] = shared("w1_q%d%d" % (g, a), "x0" if (g, a) == (0, 1) else "w1_q%d%d" % (g, a), [P, KP], U32)
            nc.vector.quantize_mx(out=w1_q[g][a][:].bitcast(FP8X4), scales=w1_s[g][a][:], in_=w1_b[g][a][:])

        v_s = held("v_s", [P, S], U8)
        v_w0 = held("v_w0", [P, S], U32)
        v_w1 = [held("v_w1%d" % jh, [P, N], U32) for jh in range(2)]
        w4_p = held("w4_p", [P, 2, 2 * H], U8)
        w4_s = held("w4_s", [P, 2 * H], U8)
        half_b = held("half_b", [P, 2 * PACK], F32)

        nc.vector.tensor_scalar(half_b[:], b1_t[:].rearrange("p g t -> p (g t)"), 0.5, None, ALU.mult)
        load_words(0, "x2")
        w4_s_raw = shared("w4_s_raw", "x5", [P, 2 * H], U8)
        nc.vector.memset(w4_s_raw[:].bitcast(I32), 0)
        load_scale_rows(nc.sync, w4_s_raw, w4_scales)
        for a in range(2):
            nc.vector.tensor_copy(
                w4_p[:, a, :].rearrange("p (g t m b) -> p g m t b", g=2, t=PACK, b=2),
                w4_raw[:, a, :].rearrange("p (g m t b) -> p g m t b", g=2, t=PACK, b=2),
            )
        cast_w1(0, 0, True)
        load_words(1, "x3")
        cast_w1(0, 1, True)
        quant_w1(0, 0)
        load_w1(1, 0, "w1_b0")
        load_words2(0, "x4")
        nc.vector.tensor_copy(v_s[:], tab_s[:].indirect(offs_t[:]))
        for q in range(4):
            nc.sync.dma_start(v_s1[32 * q : 32 * q + 4, :].bitcast(I32), v_s[32 * q + 4 : 32 * q + 8, :].bitcast(I32))
        quant_w1(0, 1)
        load_w1(1, 1, "w1_b1")
        nc.vector.tensor_copy(v_w0[:], tab_w[0][:].bitcast(U32).indirect(offs_t[:]))
        load_words2(1, "x2")
        def deal_w4_scales(g):
            nc.vector.tensor_copy(
                w4_s[:].rearrange("p (a g t m) -> p g a m t", a=2, g=2, t=PACK)[:, g],
                w4_s_raw[:].rearrange("p (a g m t) -> p g a m t", a=2, g=2, t=PACK)[:, g],
            )

        deal_w4_scales(0)
        for jh in range(2):
            nc.vector.tensor_copy(v_w1[jh][:], tab_w[1][:].bitcast(U32).indirect(offs_t[:, 32 * jh : 32 * (jh + 1)]))
        deal_w4_scales(1)
        tab2_s = shared("tab2_s", "x5", [P, T3], U8)
        nc.vector.memset(tab2_s[:].bitcast(I32), 0)
        for q in range(4):
            nc.sync.dma_start(tab2_s[32 * q : 32 * q + 8, :].bitcast(I32), tab2_scales[:, 4 * q : 4 * q + 4, :].bitcast(I32))
        prior_t = shared("prior_t", "x3", [P, 4, NP], F32)
        nc.sync.dma_start(prior_t[:], prior.rearrange("(c p) n -> p c n", p=P))

        v2_w = [held("v2_w%d" % a, [P, S2], U32) for a in range(2)]
        v2_s = held("v2_s", [P, S2], U8)
        h_q = [[held("h_q%d%d" % (g, jh), [P, N], U32) for jh in range(2)] for g in range(2)]
        h_s = [[held("h_s%d%d" % (g, jh), [P, N], U8) for jh in range(2)] for g in range(2)]
        e_t = [held("e_t%d" % c, [P, S], F32) for c in range(4)]

        def v_words(a, jh):
            return (v_w0[:, N * jh : N * (jh + 1)] if a == 0 else v_w1[jh][:]).bitcast(FP8X4)

        UNITS = [(g, jh, t) for g in range(2) for jh in range(2) for t in range(PACK)]
        sines, squares, prods, planes, woven = {}, {}, {}, {}, {}

        def phase(u):
            g, jh, t = UNITS[u]
            js = slice(N * jh, N * (jh + 1))
            ms = slice(P * t, P * (t + 1))
            pa = psum.tile([P, N], F32, name="pa", bufs=3)
            for a in range(2):
                nc.tensor.matmul_mx(
                    out=pa[:], lhsT=w1_q[g][a][:, ms].bitcast(FP8X4), lhsT_scale=w1_s[g][a][:, ms],
                    rhs=v_words(a, jh), rhs_scale=v_s[4 * a :, js], start=(a == 0), stop=(a == 1),
                )
            sines[u] = ring.tile([P, N], F32, name="sn", bufs=3)
            nc.scalar.activation(sines[u][:], pa[:], ACT.Sin, bias=half_b[:, PACK * g + t : PACK * g + t + 1], scale=0.5)

        def square(u):
            squares[u] = ring.tile([P, N], F32, name="sq", bufs=6)
            nc.scalar.activation(squares[u][:], sines[u][:], ACT.Square)

        def amplitude(u):
            g, jh, t = UNITS[u]
            js = slice(N * jh, N * (jh + 1))
            pb = psum.tile([P, N], F32, name="pb", bufs=3)
            for a in range(2):
                col = H * a + KP * g + P * t
                nc.tensor.matmul_mx(
                    out=pb[:], lhsT=w4_p[:, a, 2 * (KP * g + P * t) : 2 * (KP * g + P * (t + 1))].bitcast(FP4X4),
                    lhsT_scale=w4_s[:, col : col + P],
                    rhs=v_words(a, jh), rhs_scale=(v_s if a == 0 else v_s1)[:, js], start=(a == 0), stop=(a == 1),
                )
            prods[u] = pb

        def combine(u):
            g, jh, t = UNITS[u]
            if t == 0:
                planes[2 * g + jh] = ring.tile([P, PACK, N], BF16, name="planes", bufs=2, align_bytes=64)
            nc.vector.scalar_tensor_tensor(planes[2 * g + jh][:, t, :], squares[u][:], 0.5, prods[u][:], ALU.subtract, ALU.mult)

        def weave(q, j0=0, j1=N):
            if j0 == 0:
                woven[q] = ring.tile([P, PACK * N], BF16, name="woven", bufs=2, align_bytes=64)
            nc.vector.tensor_copy(
                woven[q][:, PACK * j0 : PACK * j1].rearrange("p (c i t) -> p c t i", i=8, t=PACK),
                planes[q][:, :, j0:j1].rearrange("p t (c i) -> p c t i", i=8),
            )

        def quant_h(q, j0=0, j1=N):
            g, jh = divmod(q, 2)
            nc.vector.quantize_mx(
                out=h_q[g][jh][:, j0:j1].bitcast(FP8X4), scales=h_s[g][jh][:, j0:j1], in_=woven[q][:, PACK * j0 : PACK * j1]
            )

        def gather_v2(a):
            nc.vector.tensor_copy(v2_w[a][:], tab2_w[a][:].bitcast(U32).indirect(offs2_t[:]))

        def gather_v2_s():
            nc.vector.tensor_copy(v2_s[:], tab2_s[:].indirect(offs2_t[:]))

        def scores(c, jh, on_scalar, j0=0, j1=N):
            pe = psum.tile([P, j1 - j0], F32, name="pe", bufs=2)
            ms = slice(P * c, P * (c + 1))
            for a in range(2):
                nc.tensor.matmul_mx(
                    out=pe[:], lhsT=v2_w[a][:, ms].bitcast(FP8X4), lhsT_scale=v2_s[4 * a :, ms],
                    rhs=h_q[a][jh][:, j0:j1].bitcast(FP8X4), rhs_scale=h_s[a][jh][:, j0:j1], start=(a == 0), stop=(a == 1),
                )
            if on_scalar:
                nc.scalar.copy(e_t[c][:, N * jh + j0 : N * jh + j1], pe[:])
            else:
                nc.vector.tensor_copy(e_t[c][:, N * jh + j0 : N * jh + j1], pe[:])

        half = N // 2
        extras = {
            0: [lambda: cast_w1(1, 0, False)],
            1: [lambda: quant_w1(1, 0), lambda: cast_w1(1, 1, True)],
            2: [lambda: gather_v2(0)],
            3: [lambda: quant_w1(1, 1)],
            4: [lambda: weave(0)],
            5: [lambda: quant_h(0)],
            6: [lambda: gather_v2(1)],
            8: [lambda: weave(1)],
            9: [lambda: quant_h(1)],
            10: [gather_v2_s],
            12: [lambda: weave(2)],
            13: [lambda: quant_h(2)],
            14: [lambda: scores(0, 0, True), lambda: scores(1, 0, True)],
            15: [lambda: weave(3, 0, half), lambda: weave(3, half, N), lambda: quant_h(3, 0, half), lambda: scores(0, 1, True, 0, half),
                 lambda: quant_h(3, half, N), lambda: scores(0, 1, True, half, N)],
        }
        LEAD = 4
        for step in range(-LEAD, 16):
            if step + LEAD < 16:
                phase(step + LEAD)
            if 0 <= step + LEAD - 1 < 16:
                square(step + LEAD - 1)
            if 0 <= step + 1 < 16:
                amplitude(step + 1)
            if step >= 0:
                combine(step)
                for f in extras.get(step, []):
                    f()

        rho_t = shared("rho_t", "w1_b10", [P, 4], F32)
        with nc.allow_non_contiguous_dma(reason="one value a partition"):
            nc.sync.dma_start(rho_t[:], rho.rearrange("(c p) -> p c", p=P))
        picked, right, diff, dist = {}, {}, {}, {}

        def pick_right(c):
            picked[c] = ring.tile([P, NP], F32, name="r", bufs=2)
            nc.vector.tensor_copy(picked[c][:], e_t[c][:].indirect(pos2_t[:]))

        def balance(c):
            right[c] = ring.tile([P, NP], F32, name="rr")
            nc.scalar.activation(right[c][:], picked[c][:], ACT.Copy, scale=rho_t[:, c : c + 1])

        def pick_left(c):
            diff[c] = ring.tile([P, NP], F32, name="d", bufs=2)
            nc.vector.tensor_tensor(diff[c][:], e_t[c][:].indirect(pos1_t[:]), right[c][:], ALU.subtract)

        def distance(c):
            dist[c] = ring.tile([P, NP], F32, name="dd")
            nc.scalar.activation(dist[c][:], diff[c][:], ACT.Abs, scale=2.0)

        def store(c):
            o = ring.tile([P, NP], F32, name="o", bufs=2)
            nc.vector.tensor_tensor(o[:], prior_t[:, c, :], dist[c][:], ALU.subtract)
            nc.sync.dma_start(out[P * c : P * (c + 1), :], o[:])

        pick_right(0)
        for c in range(6):
            if c + 1 < 4:
                if c + 1 >= 2:
                    scores(c + 1, 0, True)
                scores(c + 1, 1, True)
                pick_right(c + 1)
            if c < 4:
                balance(c)
            if 1 <= c < 5:
                distance(c - 1)
            if c < 4:
                pick_left(c)
            if 1 <= c < 5:
                store(c - 1)
